import numpy as np
import ml_dtypes


def mxq(x, axis, fmt="e4m3"):
    dtype, down = {"e4m3": (ml_dtypes.float8_e4m3fn, 7), "e5m2": (ml_dtypes.float8_e5m2, 14)}[fmt]
    v = np.moveaxis(np.asarray(x, np.float32).astype(ml_dtypes.bfloat16).astype(np.float64), axis, -1)
    blocks = v.reshape(v.shape[:-1] + (-1, 32))
    amax = np.abs(blocks).max(-1, keepdims=True)
    byte = np.maximum(np.where(amax > 0, np.frexp(amax)[1] - 1 + 127, 0) - down, 1)
    scale = np.exp2(byte - 127.0)
    codes = (blocks / scale).astype(np.float32).astype(dtype).astype(np.float64)
    return np.moveaxis((codes * scale).reshape(v.shape), -1, axis)


WIDE = False


def mx_kscale(k):
    if not WIDE:
        return np.ones(k)
    levels = np.array([10, -10, 5, -5, 0])
    if k % 512:
        return np.exp2(np.random.permutation(np.resize(levels, k // 32))).repeat(32)
    a = np.empty((k // 512, 16))
    for p in range(k // 512):
        a[p, :8] = np.random.permutation(np.resize(levels, 8))
        for g in range(8):
            far = levels[np.abs(levels - a[p, g]) >= 10]
            a[p, g + 8] = far[np.random.randint(len(far))]
    return np.exp2(a.ravel()).repeat(32)


def f64(x):
    return np.asarray(x).astype(np.float64)


def striped(idx):
    return np.tile(idx.reshape(-1, 16).T, (8, 1)).astype(np.uint16)


def unstriped(offs):
    return offs[:16].T.reshape(-1).astype(np.int64)


def pack_weight(w):
    k, n = w.shape
    w = f64(np.asarray(w, np.float32).astype(ml_dtypes.bfloat16)).reshape(k // 32, 32, n)
    amax = np.abs(w).max(1)
    byte = np.clip(np.where(amax > 0, np.frexp(amax)[1] - 1 + 127 - 7, 1), 1, 254)
    scaled = (w * np.exp2(127.0 - byte)[:, None, :]).reshape(k, n).astype(np.float32)
    words = np.ascontiguousarray(scaled.reshape(k // 512, 128, 4, n).transpose(0, 1, 3, 2)).astype(ml_dtypes.float8_e4m3fn).view(np.uint8)
    return words, np.ascontiguousarray(byte.astype(np.uint8).reshape(k // 512, 16, n))


def unpack_weight(words, scales):
    g, p, n, _ = words.shape
    vals = np.ascontiguousarray(words).view(ml_dtypes.float8_e4m3fn).astype(np.float64) * np.repeat(np.exp2(scales.astype(np.float64) - 127.0), 8, axis=1)[..., None]
    return vals.transpose(0, 1, 3, 2).reshape(g * 512, n)


K, T, S, N, W = 1024, 4096, 1024, 512, 2048
P = 2 ** 7


def setup_inputs():
    n = np.random.standard_normal
    s = mx_kscale(K)[:, None]
    c = mx_kscale(S)
    packed_xT = pack_weight(n((K, T)) * s)
    packed_eT = pack_weight(n((K, W)) * s)
    return {
        "x_words": packed_xT[0],
        "x_scales": packed_xT[1],
        "e_words": packed_eT[0],
        "e_scales": packed_eT[1],
        "wa": (n((K, N)) / np.sqrt(K) / s).astype(np.float32),
        "mean": (np.tile(0.2 * n(N), (P, 1))).astype(np.float32),
        "wgt": (np.random.uniform(0.5, 1.0, (S, 1)) * c[:, None] / np.sqrt(S)).astype(np.float32),
        "wb": (n((K, N)) / np.sqrt(K) / s).astype(np.float32),
        "inv": (np.random.uniform(0.6, 1.4, (S, 1)) / c[:, None]).astype(np.float32),
        "goal": (np.eye(N) * np.random.uniform(0.8, 1.2, N)).astype(np.float32),
        "lam": (np.random.uniform(0.1, 1.0, (N, N))).astype(np.float32),
        "offs": striped(np.random.permutation(T)[:S]),
        "par": striped(np.random.permutation(W)[:S]),
    }


def reference(x_words, x_scales, e_words, e_scales, wa, mean, wgt, wb, inv, goal, lam, offs, par):
    xq = unpack_weight(x_words, x_scales)[:, unstriped(offs)]
    waq = mxq(f64(wa), 0, "e4m3")
    a = f64(wgt) * ((xq.T @ waq) - f64(mean)[:1])
    e_par = unpack_weight(e_words, e_scales)[:, unstriped(par)]
    wbq = mxq(f64(wb), 0, "e4m3")
    vv = f64(inv) * (e_par.T @ wbq)
    z = mxq(a, 0, "e4m3").T @ mxq(vv, 0, "e4m3")
    dd = z - f64(goal)
    return dd * f64(lam)

@@ -1,0 +1,262 @@
+from contextlib import ExitStack
+
+import concourse.mybir as mybir
+from concourse.masks import make_identity
+
+K, T, S, N, W = 1024, 4096, 1024, 512, 2048
+P = 128
+PACK = 4
+PASSES = K // (P * PACK)
+HALF = 512
+HALVES = S // HALF
+TILES = N // P
+
+F32 = mybir.dt.float32
+BF16 = mybir.dt.bfloat16
+I32 = mybir.dt.int32
+U32 = mybir.dt.uint32
+U16 = mybir.dt.uint16
+U8 = mybir.dt.uint8
+FP8X4 = mybir.dt.float8_e4m3fn_x4
+MULT = mybir.AluOpType.mult
+SUB = mybir.AluOpType.subtract
+COPY = mybir.ActivationFunctionType.Copy
+
+FLOPS = 2 * S * K * N * 2 + 2 * S * N * N
+BYTES = K * (T + W) * 33 // 32 + 4 * (2 * K * N + 2 * N + 2 * S + 2 * N * N) + 2 * 2 * P * S // 16
+
+
+def tile_picked_ybarlow_grad_p_kernel(
+    tc, x_words, x_scales, e_words, e_scales, wa, mean, wgt, wb, inv, goal, lam, offs, par, out
+):
+    nc = tc.nc
+    with ExitStack() as ctx:
+        keep = ctx.enter_context(tc.tile_pool(name="keep", bufs=1))
+        psum = ctx.enter_context(tc.psum_pool(name="psum", bufs=1))
+
+        def sb(name, shape, dtype, tag=""):
+            return keep.tile(shape, dtype, name=name, tag=tag or name, align_bytes=64)
+
+        def bank(tag, bufs):
+            return psum.tile([P, HALF], F32, name=tag, bufs=bufs)
+
+        par_sb = keep.tile([P, S // 16], U16, name="par_sb")
+        offs_sb = keep.tile([P, S // 16], U16, name="offs_sb")
+
+        def scale_table(name, columns, engine):
+            table = sb(name, [P, columns // 4], I32)
+            engine.memset(table[:], 0)
+            return table
+
+        def load_scales(table, scales, first_row):
+            for q in range(4):
+                row = 32 * q + first_row
+                nc.sync.dma_start(out=table[row : row + 4 * PASSES, :], in_=scales[:, 4 * q : 4 * q + 4, :].bitcast(I32))
+
+        def word_table(name, words, columns, pieces):
+            table = sb(name, [P, columns], I32)
+            view = words.rearrange("p n t -> p (n t)").bitcast(I32)
+            step = columns // pieces
+            return table, [(table[:, a * step : (a + 1) * step], view[:, a * step : (a + 1) * step]) for a in range(pieces)]
+
+        def load(pairs):
+            for dst, src in pairs:
+                nc.sync.dma_start(out=dst, in_=src)
+
+        def gather_words(name, window, offsets, halves, tag=""):
+            picked = sb(name, [P, halves * HALF], U32, tag)
+            dealt = picked[:].rearrange("p (h s g r) -> p h g s r", h=halves, s=4, r=8)
+            nc.vector.tensor_copy(out=dealt, in_=window[:].bitcast(U32).indirect(offsets))
+            return picked
+
+        def gather_scales(name, window, offsets, tag=""):
+            picked = sb(name + "_listed", [P, S], U8, tag)
+            nc.vector.tensor_copy(out=picked[:], in_=window[:].bitcast(U8).indirect(offsets))
+            dealt = sb(name, [P, S], U8)
+            nc.vector.tensor_copy(
+                out=dealt[:].bitcast(I32).rearrange("p (h s g w) -> p h s g w", h=HALVES, s=4, w=2),
+                in_=picked[:].bitcast(I32).rearrange("p (h g s w) -> p h s g w", h=HALVES, s=4, w=2),
+            )
+            return dealt
+
+        def load_weight(name, w, g, c0, c1, pieces=1):
+            raw = sb(name, [P, PACK, c1 - c0], F32)
+            rows = w[g * P * PACK : (g + 1) * P * PACK, c0:c1].rearrange("(p j) n -> p j n", j=PACK)
+            step = PACK // pieces
+            load([(raw[:, a * step : (a + 1) * step, :], rows[:, a * step : (a + 1) * step, :]) for a in range(pieces)])
+            return raw
+
+        def quantize(name, grouped, columns):
+            codes = sb(name + "_codes", [P, columns], U32)
+            scales = sb(name + "_scales", [P, columns], U8)
+            nc.vector.quantize_mx(out=codes[:].bitcast(FP8X4), scales=scales[:], in_=grouped)
+            return codes, scales
+
+        def round_weight(grouped, raw, c0, c1, copy):
+            copy(
+                out=grouped[:, c0 * PACK : c1 * PACK].rearrange("p (c i j) -> p c j i", i=4, j=PACK),
+                in_=raw[:, :, c0:c1].rearrange("p j (c i) -> p c j i", i=4),
+            )
+
+        def quantize_weight(name, raw, on_vector=0, tag=""):
+            grouped = sb(name + "_bf16", [P, N * PACK], BF16, tag)
+            if on_vector < N:
+                round_weight(grouped, raw, 0, N - on_vector, nc.scalar.copy)
+            if on_vector:
+                round_weight(grouped, raw, N - on_vector, N, nc.vector.tensor_copy)
+            return quantize(name, grouped[:], N)
+
+        e_scale_table = scale_table("e_scale_table", W, nc.vector)
+        x_scale_table = scale_table("x_scale_table", T, nc.vector)
+        small_rows = sb("small_rows", [P, HALVES * P], F32)
+        nc.gpsimd.memset(small_rows[:], 0.0)
+        wgt_cols = sb("wgt_cols", [P, S // P], F32)
+        ident = sb("ident", [P, P], F32)
+        make_identity(nc, ident[:])
+        nc.gpsimd.dma_start(
+            out=small_rows[0:4, :].rearrange("s (g r) -> s g r", r=8),
+            in_=inv.rearrange("(g s r) o -> s g (r o)", s=4, r=8),
+        )
+        nc.gpsimd.dma_start(out=small_rows[4 : 4 + TILES, 0:P], in_=mean[0:1, :].rearrange("o (c n) -> (o c) n", c=TILES))
+
+        e_loads = [word_table("e_table%d" % g, e_words[g], W, 2) for g in range(PASSES)]
+        x_loads = [word_table("x_table%d" % g, x_words[g], T, 1) for g in range(PASSES)]
+        e_tables = [table for table, pairs in e_loads]
+        x_tables = [table for table, pairs in x_loads]
+        nc.sync.dma_start(out=par_sb[:], in_=par)
+        load(e_loads[0][1])
+        nc.sync.dma_start(out=wgt_cols[:], in_=wgt.rearrange("(p c) o -> p (c o)", p=P))
+        load(e_loads[1][1])
+        wb_raw = [load_weight("wb_raw0", wb, 0, 0, N, 2)]
+        load_scales(e_scale_table, e_scales, 8)
+        wb_raw.append(load_weight("wb_raw1", wb, 1, 0, N))
+        wa_raw0 = load_weight("wa_raw0", wa, 0, 0, N)
+        nc.sync.dma_start(out=offs_sb[:], in_=offs)
+        load_scales(x_scale_table, x_scales, 0)
+        load(x_loads[0][1])
+        load(x_loads[1][1])
+        wa_raw1 = [load_weight("wa_raw1_%d" % a, wa, 1, a * 2 * P, (a + 1) * 2 * P) for a in range(2)]
+        goal_sb = []
+        lam_sb = []
+        for c in range(TILES):
+            rows = slice(c * P, (c + 1) * P)
+            lam_sb.append(sb("lam%d" % c, [P, N], F32))
+            nc.sync.dma_start(out=lam_sb[c][:], in_=lam[rows, :])
+            goal_sb.append(sb("goal%d" % c, [P, P], F32))
+            nc.sync.dma_start(out=goal_sb[c][:], in_=goal[rows, rows])
+
+        wgt_row = sb("wgt_row", [P, S], F32)
+        wgt_view = wgt_row[:].rearrange("q (h u g b c e) -> q b u h g c e", h=HALVES, u=2, b=2, c=4, e=2)
+        for b in range(2):
+            spread = bank("mm", 4)
+            for c in range(4):
+                col = 4 * b + c
+                nc.tensor.transpose(spread[:, c * P : (c + 1) * P], wgt_cols[:, col : col + 1].to_broadcast([P, P]), ident[:])
+            spread_view = spread[:].rearrange("q (c h g e u) -> q u h g c e", c=4, h=HALVES, e=2, u=2)
+            for u in range(2):
+                nc.scalar.copy(out=wgt_view[:, b, u], in_=spread_view[:, u])
+
+        small_turned = bank("turn", 2)
+        for h in range(HALVES):
+            nc.tensor.transpose(small_turned[:, h * P : (h + 1) * P], small_rows[:, h * P : (h + 1) * P], ident[:])
+        small_cols = sb("small_cols", [P, HALVES, 8], F32)
+        nc.scalar.copy(out=small_cols[:], in_=small_turned[:, 0 : HALVES * P].rearrange("p (h r) -> p h r", h=HALVES)[:, :, 0:8])
+
+        def mx(acc, lhs, lhs_scale, rhs, rhs_scale, step, steps):
+            nc.tensor.matmul_mx(
+                out=acc,
+                lhsT=lhs.bitcast(FP8X4),
+                lhsT_scale=lhs_scale,
+                rhs=rhs.bitcast(FP8X4),
+                rhs_scale=rhs_scale,
+                start=(step == 0),
+                stop=(step == steps - 1),
+            )
+
+        e_picked = [gather_words("e_picked%d" % g, e_tables[g], par_sb[:], HALVES) for g in range(PASSES)]
+        e_picked_scales = gather_scales("e_picked_scales", e_scale_table, par_sb[:])
+        wb_q = [quantize_weight("wb%d" % g, wb_raw[g], g * N // 2) for g in range(PASSES)]
+        x_picked_scales = gather_scales("x_picked_scales", x_scale_table, offs_sb[:], "wb1_bf16")
+        wa_q0 = quantize_weight("wa0", wa_raw0, N, "wb1_bf16")
+        x_picked0 = gather_words("x_picked0", x_tables[0], offs_sb[:], HALVES, "wb1_bf16")
+
+        vv_q = []
+        for h in range(HALVES):
+            pairs = sb("vv_pairs%d" % h, [P, 2, N, 2], BF16)
+            for s in range(4):
+                acc = bank("mm", 4)
+                ts = slice(h * HALF + s * P, h * HALF + (s + 1) * P)
+                for g in range(PASSES):
+                    mx(acc[:], e_picked[g][:, ts], e_picked_scales[8 + 4 * g : P, ts], wb_q[g][0][:], wb_q[g][1][:], g, PASSES)
+                nc.scalar.activation(out=pairs[:, s % 2, :, s // 2], in_=acc[:], func=COPY, scale=small_cols[:, h, s : s + 1])
+            grouped = sb("vv_grouped%d" % h, [P, N * PACK], BF16)
+            nc.vector.tensor_copy(
+                out=grouped[:].bitcast(F32).rearrange("p (m u) -> p m u", u=2),
+                in_=pairs[:].rearrange("p u m e -> p u (m e)").bitcast(F32).rearrange("p u m -> p m u"),
+            )
+            vv_q.append(quantize("vv%d" % h, grouped[:], N))
+
+        cols_per_half = HALF // 16
+        x_picked1 = [
+            gather_words("x_picked1_%d" % h, x_tables[1], offs_sb[:, h * cols_per_half : (h + 1) * cols_per_half], 1, ("vv_grouped0", "vv_pairs0")[h])
+            for h in range(HALVES)
+        ]
+
+        wa1_bf16 = [sb("wa1_bf16_%d" % a, [P, 2 * P * PACK], BF16, ("vv_pairs1", "vv_grouped1")[a]) for a in range(2)]
+
+        def project(c):
+            grouped = wa1_bf16[c // 2]
+            round_weight(grouped, wa_raw1[c // 2], (c % 2) * P, (c % 2 + 1) * P, nc.scalar.copy)
+            wa_q1 = quantize("wa1_%d" % c, grouped[:, (c % 2) * HALF : (c % 2 + 1) * HALF], P)
+            cs = slice(c * P, (c + 1) * P)
+            halves = []
+            for h in range(HALVES):
+                acc = bank("mm", 4)
+                ts = slice(h * HALF, (h + 1) * HALF)
+                mx(acc[:], wa_q0[0][:, cs], wa_q0[1][:, cs], x_picked0[:, ts], x_picked_scales[0:P, ts], 0, PASSES)
+                mx(acc[:], wa_q1[0][:], wa_q1[1][:], x_picked1[h][:], x_picked_scales[4:P, ts], 1, PASSES)
+                at = sb("aT_%d_%d" % (c, h), [P, HALF], BF16)
+                nc.vector.scalar_tensor_tensor(
+                    out=at[:].rearrange("i (q e) -> i q e", e=2),
+                    in0=acc[:].rearrange("i (e q) -> i q e", e=2),
+                    scalar=small_cols[:, 0, 4 + c : 5 + c],
+                    in1=wgt_row[:, ts].rearrange("i (q e) -> i q e", e=2),
+                    op0=SUB,
+                    op1=MULT,
+                )
+                halves.append(at)
+            return halves
+
+        def turn(c, halves):
+            turned = bank("turn", 2)
+            for h in range(HALVES):
+                words = halves[h][:].bitcast(F32)
+                for u in range(2):
+                    slot = 2 * h + u
+                    nc.tensor.transpose(turned[:, slot * P : (slot + 1) * P], words[:, u * P : (u + 1) * P], ident[:])
+            a_grouped = sb("a_grouped%d" % c, [P, HALVES * P * PACK], BF16)
+            nc.scalar.copy(
+                out=a_grouped[:].bitcast(F32).rearrange("p (h i u) -> p h i u", h=HALVES, u=2),
+                in_=turned[:].rearrange("p (h u i) -> p h i u", h=HALVES, u=2),
+            )
+            return a_grouped
+
+        def correlate(c, a_grouped):
+            a_codes, a_scales = quantize("a%d" % c, a_grouped[:], HALVES * P)
+            z = bank("z", 2)
+            for h in range(HALVES):
+                hs = slice(h * P, (h + 1) * P)
+                mx(z[:], a_codes[:, hs], a_scales[:, hs], vv_q[h][0][:], vv_q[h][1][:], h, HALVES)
+            return z
+
+        def finish(c, z):
+            diag = slice(c * P, (c + 1) * P)
+            goal_lam = sb("goal_lam%d" % c, [P, P], F32)
+            nc.gpsimd.tensor_tensor(out=goal_lam[:], in0=goal_sb[c][:], in1=lam_sb[c][:, diag], op=MULT)
+            res = sb("res%d" % c, [P, N], F32)
+            nc.vector.tensor_tensor(out=res[:], in0=z[:], in1=lam_sb[c][:], op=MULT)
+            nc.vector.tensor_tensor(out=res[:, diag], in0=res[:, diag], in1=goal_lam[:], op=SUB)
+            nc.sync.dma_start(out=out[diag, :], in_=res[:])
+
+        for c in range(TILES):
+            finish(c, correlate(c, turn(c, project(c))))

@@ -53,8 +53,8 @@ def tile_picked_ybarlow_grad_p_kernel(
                 row = 32 * q + first_row
                 nc.sync.dma_start(out=table[row : row + 4 * PASSES, :], in_=scales[:, 4 * q : 4 * q + 4, :].bitcast(I32))
 
-        def word_table(name, words, columns, pieces):
-            table = sb(name, [P, columns], I32)
+        def word_table(name, words, columns, pieces, tag=""):
+            table = sb(name, [P, columns], I32, tag)
             view = words.rearrange("p n t -> p (n t)").bitcast(I32)
             step = columns // pieces
             return table, [(table[:, a * step : (a + 1) * step], view[:, a * step : (a + 1) * step]) for a in range(pieces)]
@@ -79,15 +79,15 @@ def tile_picked_ybarlow_grad_p_kernel(
             )
             return dealt
 
-        def load_weight(name, w, g, c0, c1, pieces=1):
-            raw = sb(name, [P, PACK, c1 - c0], F32)
+        def load_weight(name, w, g, c0, c1, pieces=1, tag=""):
+            raw = sb(name, [P, PACK, c1 - c0], F32, tag)
             rows = w[g * P * PACK : (g + 1) * P * PACK, c0:c1].rearrange("(p j) n -> p j n", j=PACK)
             step = PACK // pieces
             load([(raw[:, a * step : (a + 1) * step, :], rows[:, a * step : (a + 1) * step, :]) for a in range(pieces)])
             return raw
 
-        def quantize(name, grouped, columns):
-            codes = sb(name + "_codes", [P, columns], U32)
+        def quantize(name, grouped, columns, tag=""):
+            codes = sb(name + "_codes", [P, columns], U32, tag)
             scales = sb(name + "_scales", [P, columns], U8)
             nc.vector.quantize_mx(out=codes[:].bitcast(FP8X4), scales=scales[:], in_=grouped)
             return codes, scales
@@ -106,7 +106,7 @@ def tile_picked_ybarlow_grad_p_kernel(
                 round_weight(grouped, raw, N - on_vector, N, nc.vector.tensor_copy)
             return quantize(name, grouped[:], N)
 
-        e_scale_table = scale_table("e_scale_table", W, nc.vector)
+        e_scale_table = scale_table("e_scale_table", W, nc.gpsimd)
         x_scale_table = scale_table("x_scale_table", T, nc.vector)
         small_rows = sb("small_rows", [P, HALVES * P], F32)
         nc.gpsimd.memset(small_rows[:], 0.0)
@@ -119,31 +119,18 @@ def tile_picked_ybarlow_grad_p_kernel(
         )
         nc.gpsimd.dma_start(out=small_rows[4 : 4 + TILES, 0:P], in_=mean[0:1, :].rearrange("o (c n) -> (o c) n", c=TILES))
 
-        e_loads = [word_table("e_table%d" % g, e_words[g], W, 2) for g in range(PASSES)]
-        x_loads = [word_table("x_table%d" % g, x_words[g], T, 1) for g in range(PASSES)]
+        e_loads = [word_table("e_table%d" % g, e_words[g], W, 4) for g in range(PASSES)]
         e_tables = [table for table, pairs in e_loads]
-        x_tables = [table for table, pairs in x_loads]
+        nc.sync.dma_start(out=wgt_cols[:], in_=wgt.rearrange("(p c) o -> p (c o)", p=P))
         nc.sync.dma_start(out=par_sb[:], in_=par)
         load(e_loads[0][1])
-        nc.sync.dma_start(out=wgt_cols[:], in_=wgt.rearrange("(p c) o -> p (c o)", p=P))
         load(e_loads[1][1])
         wb_raw = [load_weight("wb_raw0", wb, 0, 0, N, 2)]
         load_scales(e_scale_table, e_scales, 8)
         wb_raw.append(load_weight("wb_raw1", wb, 1, 0, N))
+        load_scales(x_scale_table, x_scales, 0)
         wa_raw0 = load_weight("wa_raw0", wa, 0, 0, N)
         nc.sync.dma_start(out=offs_sb[:], in_=offs)
-        load_scales(x_scale_table, x_scales, 0)
-        load(x_loads[0][1])
-        load(x_loads[1][1])
-        wa_raw1 = [load_weight("wa_raw1_%d" % a, wa, 1, a * 2 * P, (a + 1) * 2 * P) for a in range(2)]
-        goal_sb = []
-        lam_sb = []
-        for c in range(TILES):
-            rows = slice(c * P, (c + 1) * P)
-            lam_sb.append(sb("lam%d" % c, [P, N], F32))
-            nc.sync.dma_start(out=lam_sb[c][:], in_=lam[rows, :])
-            goal_sb.append(sb("goal%d" % c, [P, P], F32))
-            nc.sync.dma_start(out=goal_sb[c][:], in_=goal[rows, rows])
 
         wgt_row = sb("wgt_row", [P, S], F32)
         wgt_view = wgt_row[:].rearrange("q (h u g b c e) -> q b u h g c e", h=HALVES, u=2, b=2, c=4, e=2)
@@ -175,21 +162,35 @@ def tile_picked_ybarlow_grad_p_kernel(
 
         e_picked = [gather_words("e_picked%d" % g, e_tables[g], par_sb[:], HALVES) for g in range(PASSES)]
         e_picked_scales = gather_scales("e_picked_scales", e_scale_table, par_sb[:])
-        wb_q = [quantize_weight("wb%d" % g, wb_raw[g], g * N // 2) for g in range(PASSES)]
+        wb_q = [quantize_weight("wb0", wb_raw[0], 0, "wgt_cols"), quantize_weight("wb1", wb_raw[1], N // 2)]
+        wa0_bf16 = sb("wa0_bf16", [P, N * PACK], BF16)
+        round_weight(wa0_bf16, wa_raw0, 0, N, nc.scalar.copy)
         x_picked_scales = gather_scales("x_picked_scales", x_scale_table, offs_sb[:], "wb1_bf16")
-        wa_q0 = quantize_weight("wa0", wa_raw0, N, "wb1_bf16")
+        wa_q0 = quantize("wa0", wa0_bf16[:], N, "x_scale_table")
+        x_loads = [word_table("x_table%d" % g, x_words[g], T, 1, "e_table%d" % g) for g in range(PASSES)]
+        x_tables = [table for table, pairs in x_loads]
+        load(x_loads[0][1])
+        load(x_loads[1][1])
+        goal_sb = sb("goal_sb", [P, TILES, P], F32, "e_scale_table")
+        for c in range(TILES):
+            nc.sync.dma_start(out=goal_sb[:, c, :], in_=goal[c * P : (c + 1) * P, c * P : (c + 1) * P])
+        wa_raw1 = [load_weight("wa_raw1_%d" % a, wa, 1, a * 2 * P, (a + 1) * 2 * P, 1, "wb_raw%d" % a) for a in range(2)]
+        lam_pairs = [sb("lam%d" % a, [P, 2, N], F32, ("wgt_cols", "wa0_bf16")[a]) for a in range(2)]
+        for a in range(2):
+            nc.sync.dma_start(out=lam_pairs[a][:], in_=lam[a * 2 * P : (a + 1) * 2 * P, :].rearrange("(c p) m -> p c m", p=P))
+        lam_sb = [lam_pairs[c // 2][:, c % 2, :] for c in range(TILES)]
         x_picked0 = gather_words("x_picked0", x_tables[0], offs_sb[:], HALVES, "wb1_bf16")
 
         vv_q = []
         for h in range(HALVES):
-            pairs = sb("vv_pairs%d" % h, [P, 2, N, 2], BF16)
+            pairs = sb("vv_pairs%d" % h, [P, 2, N, 2], BF16, ("wa_raw0", "vv_pairs1")[h])
             for s in range(4):
                 acc = bank("mm", 4)
                 ts = slice(h * HALF + s * P, h * HALF + (s + 1) * P)
                 for g in range(PASSES):
                     mx(acc[:], e_picked[g][:, ts], e_picked_scales[8 + 4 * g : P, ts], wb_q[g][0][:], wb_q[g][1][:], g, PASSES)
                 nc.scalar.activation(out=pairs[:, s % 2, :, s // 2], in_=acc[:], func=COPY, scale=small_cols[:, h, s : s + 1])
-            grouped = sb("vv_grouped%d" % h, [P, N * PACK], BF16)
+            grouped = sb("vv_grouped%d" % h, [P, N * PACK], BF16, ("e_table0", "wa_raw0")[h])
             nc.vector.tensor_copy(
                 out=grouped[:].bitcast(F32).rearrange("p (m u) -> p m u", u=2),
                 in_=pairs[:].rearrange("p u m e -> p u (m e)").bitcast(F32).rearrange("p u m -> p m u"),
@@ -197,24 +198,25 @@ def tile_picked_ybarlow_grad_p_kernel(
             vv_q.append(quantize("vv%d" % h, grouped[:], N))
 
         cols_per_half = HALF // 16
-        x_picked1 = [
-            gather_words("x_picked1_%d" % h, x_tables[1], offs_sb[:, h * cols_per_half : (h + 1) * cols_per_half], 1, ("vv_grouped0", "vv_pairs0")[h])
-            for h in range(HALVES)
-        ]
+        x_picked1 = sb("x_picked1", [P, S], U32, "wa_raw0")
+        for h in range(HALVES):
+            dealt = x_picked1[:, h * HALF : (h + 1) * HALF].rearrange("p (s g r) -> p g s r", s=4, r=8)
+            offsets = offs_sb[:, h * cols_per_half : (h + 1) * cols_per_half]
+            nc.vector.tensor_copy(out=dealt, in_=x_tables[1][:].bitcast(U32).indirect(offsets))
 
-        wa1_bf16 = [sb("wa1_bf16_%d" % a, [P, 2 * P * PACK], BF16, ("vv_pairs1", "vv_grouped1")[a]) for a in range(2)]
+        wa1_bf16 = sb("wa1_bf16", [P, N * PACK], BF16, "vv_pairs1")
 
         def project(c):
-            grouped = wa1_bf16[c // 2]
+            grouped = wa1_bf16[:, (c // 2) * 2 * HALF : (c // 2 + 1) * 2 * HALF]
             round_weight(grouped, wa_raw1[c // 2], (c % 2) * P, (c % 2 + 1) * P, nc.scalar.copy)
-            wa_q1 = quantize("wa1_%d" % c, grouped[:, (c % 2) * HALF : (c % 2 + 1) * HALF], P)
+            wa_q1 = quantize("wa1_%d" % c, wa1_bf16[:, c * HALF : (c + 1) * HALF], P)
             cs = slice(c * P, (c + 1) * P)
             halves = []
             for h in range(HALVES):
                 acc = bank("mm", 4)
                 ts = slice(h * HALF, (h + 1) * HALF)
                 mx(acc[:], wa_q0[0][:, cs], wa_q0[1][:, cs], x_picked0[:, ts], x_picked_scales[0:P, ts], 0, PASSES)
-                mx(acc[:], wa_q1[0][:], wa_q1[1][:], x_picked1[h][:], x_picked_scales[4:P, ts], 1, PASSES)
+                mx(acc[:], wa_q1[0][:], wa_q1[1][:], x_picked1[:, ts], x_picked_scales[4:P, ts], 1, PASSES)
                 at = sb("aT_%d_%d" % (c, h), [P, HALF], BF16)
                 nc.vector.scalar_tensor_tensor(
                     out=at[:].rearrange("i (q e) -> i q e", e=2),
@@ -252,9 +254,9 @@ def tile_picked_ybarlow_grad_p_kernel(
         def finish(c, z):
             diag = slice(c * P, (c + 1) * P)
             goal_lam = sb("goal_lam%d" % c, [P, P], F32)
-            nc.gpsimd.tensor_tensor(out=goal_lam[:], in0=goal_sb[c][:], in1=lam_sb[c][:, diag], op=MULT)
+            nc.gpsimd.tensor_tensor(out=goal_lam[:], in0=goal_sb[:, c, :], in1=lam_sb[c][:, diag], op=MULT)
             res = sb("res%d" % c, [P, N], F32)
-            nc.vector.tensor_tensor(out=res[:], in0=z[:], in1=lam_sb[c][:], op=MULT)
+            nc.vector.tensor_tensor(out=res[:], in0=z[:], in1=lam_sb[c], op=MULT)
             nc.vector.tensor_tensor(out=res[:, diag], in0=res[:, diag], in1=goal_lam[:], op=SUB)
             nc.sync.dma_start(out=out[diag, :], in_=res[:])
 

@@ -127,10 +127,15 @@ def tile_picked_ybarlow_grad_p_kernel(
         load(e_loads[1][1])
         wb_raw = [load_weight("wb_raw0", wb, 0, 0, N, 2)]
         load_scales(e_scale_table, e_scales, 8)
-        wb_raw.append(load_weight("wb_raw1", wb, 1, 0, N))
-        load_scales(x_scale_table, x_scales, 0)
-        wa_raw0 = load_weight("wa_raw0", wa, 0, 0, N)
         nc.sync.dma_start(out=offs_sb[:], in_=offs)
+        wb_raw.append(load_weight("wb_raw1", wb, 1, 0, N))
+        wa_raw0 = sb("wa_raw0", [P, PACK, N], F32)
+        wa_rows0 = wa[0 : P * PACK, :].rearrange("(p j) n -> p j n", j=PACK)
+        for g in range(PASSES):
+            for q in range(4):
+                row = 32 * q + 4 * g
+                nc.sync.dma_start(out=x_scale_table[row : row + 4, :], in_=x_scales[g, 4 * q : 4 * q + 4, :].bitcast(I32))
+            nc.sync.dma_start(out=wa_raw0[:, 2 * g : 2 * g + 2, :], in_=wa_rows0[:, 2 * g : 2 * g + 2, :])
 
         wgt_row = sb("wgt_row", [P, S], F32)
         wgt_view = wgt_row[:].rearrange("q (h u g b c e) -> q b u h g c e", h=HALVES, u=2, b=2, c=4, e=2)
@@ -171,9 +176,6 @@ def tile_picked_ybarlow_grad_p_kernel(
         x_tables = [table for table, pairs in x_loads]
         load(x_loads[0][1])
         load(x_loads[1][1])
-        goal_sb = sb("goal_sb", [P, TILES, P], F32, "e_scale_table")
-        for c in range(TILES):
-            nc.sync.dma_start(out=goal_sb[:, c, :], in_=goal[c * P : (c + 1) * P, c * P : (c + 1) * P])
         wa_raw1 = [load_weight("wa_raw1_%d" % a, wa, 1, a * 2 * P, (a + 1) * 2 * P, 1, "wb_raw%d" % a) for a in range(2)]
         lam_pairs = [sb("lam%d" % a, [P, 2, N], F32, ("wgt_cols", "wa0_bf16")[a]) for a in range(2)]
         for a in range(2):
@@ -183,28 +185,29 @@ def tile_picked_ybarlow_grad_p_kernel(
 
         vv_q = []
         for h in range(HALVES):
-            pairs = sb("vv_pairs%d" % h, [P, 2, N, 2], BF16, ("wa_raw0", "vv_pairs1")[h])
+            planes = sb("vv_planes%d" % h, [P, PACK, N], BF16, ("wa_raw0", "vv_planes1")[h])
             for s in range(4):
                 acc = bank("mm", 4)
                 ts = slice(h * HALF + s * P, h * HALF + (s + 1) * P)
                 for g in range(PASSES):
                     mx(acc[:], e_picked[g][:, ts], e_picked_scales[8 + 4 * g : P, ts], wb_q[g][0][:], wb_q[g][1][:], g, PASSES)
-                nc.scalar.activation(out=pairs[:, s % 2, :, s // 2], in_=acc[:], func=COPY, scale=small_cols[:, h, s : s + 1])
-            grouped = sb("vv_grouped%d" % h, [P, N * PACK], BF16, ("e_table0", "wa_raw0")[h])
-            nc.vector.tensor_copy(
-                out=grouped[:].bitcast(F32).rearrange("p (m u) -> p m u", u=2),
-                in_=pairs[:].rearrange("p u m e -> p u (m e)").bitcast(F32).rearrange("p u m -> p m u"),
-            )
+                slot = 2 * (s % 2) + s // 2
+                nc.scalar.activation(out=planes[:, slot, :], in_=acc[:], func=COPY, scale=small_cols[:, h, s : s + 1])
+            grouped = sb("vv_grouped%d" % h, [P, N * PACK], BF16, ("e_table0", "vv_grouped1")[h])
+            round_weight(grouped, planes, 0, N, (nc.vector.tensor_copy, nc.scalar.copy)[h])
             vv_q.append(quantize("vv%d" % h, grouped[:], N))
 
+        goal_sb = sb("goal_sb", [P, TILES, P], F32, "e_picked0")
+        for c in range(TILES):
+            nc.sync.dma_start(out=goal_sb[:, c, :], in_=goal[c * P : (c + 1) * P, c * P : (c + 1) * P])
         cols_per_half = HALF // 16
-        x_picked1 = sb("x_picked1", [P, S], U32, "wa_raw0")
+        x_picked1 = sb("x_picked1", [P, S], U32, "e_table0")
         for h in range(HALVES):
             dealt = x_picked1[:, h * HALF : (h + 1) * HALF].rearrange("p (s g r) -> p g s r", s=4, r=8)
             offsets = offs_sb[:, h * cols_per_half : (h + 1) * cols_per_half]
             nc.vector.tensor_copy(out=dealt, in_=x_tables[1][:].bitcast(U32).indirect(offsets))
 
-        wa1_bf16 = sb("wa1_bf16", [P, N * PACK], BF16, "vv_pairs1")
+        wa1_bf16 = sb("wa1_bf16", [P, N * PACK], BF16, "vv_planes1")
 
         def project(c):
             grouped = wa1_bf16[:, (c // 2) * 2 * HALF : (c // 2 + 1) * 2 * HALF]

@@ -106,18 +106,13 @@ def tile_picked_ybarlow_grad_p_kernel(
                 round_weight(grouped, raw, N - on_vector, N, nc.vector.tensor_copy)
             return quantize(name, grouped[:], N)
 
-        e_scale_table = scale_table("e_scale_table", W, nc.gpsimd)
-        x_scale_table = scale_table("x_scale_table", T, nc.vector)
         small_rows = sb("small_rows", [P, HALVES * P], F32)
         nc.gpsimd.memset(small_rows[:], 0.0)
+        e_scale_table = scale_table("e_scale_table", W, nc.gpsimd)
+        x_scale_table = scale_table("x_scale_table", T, nc.vector)
         wgt_cols = sb("wgt_cols", [P, S // P], F32)
         ident = sb("ident", [P, P], F32)
         make_identity(nc, ident[:])
-        nc.gpsimd.dma_start(
-            out=small_rows[0:4, :].rearrange("s (g r) -> s g r", r=8),
-            in_=inv.rearrange("(g s r) o -> s g (r o)", s=4, r=8),
-        )
-        nc.gpsimd.dma_start(out=small_rows[4 : 4 + TILES, 0:P], in_=mean[0:1, :].rearrange("o (c n) -> (o c) n", c=TILES))
 
         e_loads = [word_table("e_table%d" % g, e_words[g], W, 4) for g in range(PASSES)]
         e_tables = [table for table, pairs in e_loads]
@@ -125,6 +120,11 @@ def tile_picked_ybarlow_grad_p_kernel(
         nc.sync.dma_start(out=par_sb[:], in_=par)
         load(e_loads[0][1])
         load(e_loads[1][1])
+        nc.sync.dma_start(
+            out=small_rows[0:4, :].rearrange("s (g r) -> s g r", r=8),
+            in_=inv.rearrange("(g s r) o -> s g (r o)", s=4, r=8),
+        )
+        nc.sync.dma_start(out=small_rows[4 : 4 + TILES, 0:P], in_=mean[0:1, :].rearrange("o (c n) -> (o c) n", c=TILES))
         wb_raw = [load_weight("wb_raw0", wb, 0, 0, N, 2)]
         load_scales(e_scale_table, e_scales, 8)
         nc.sync.dma_start(out=offs_sb[:], in_=offs)

from contextlib import ExitStack

import concourse.mybir as mybir
from concourse.masks import make_identity

K, T, S, N, W = 1024, 4096, 1024, 512, 2048
P = 128
PACK = 4
PASSES = K // (P * PACK)
HALF = 512
HALVES = S // HALF
TILES = N // P

F32 = mybir.dt.float32
BF16 = mybir.dt.bfloat16
I32 = mybir.dt.int32
U32 = mybir.dt.uint32
U16 = mybir.dt.uint16
U8 = mybir.dt.uint8
FP8X4 = mybir.dt.float8_e4m3fn_x4
MULT = mybir.AluOpType.mult
SUB = mybir.AluOpType.subtract
COPY = mybir.ActivationFunctionType.Copy

FLOPS = 2 * S * K * N * 2 + 2 * S * N * N
BYTES = K * (T + W) * 33 // 32 + 4 * (2 * K * N + 2 * N + 2 * S + 2 * N * N) + 2 * 2 * P * S // 16


def tile_picked_ybarlow_grad_p_kernel(
    tc, x_words, x_scales, e_words, e_scales, wa, mean, wgt, wb, inv, goal, lam, offs, par, out
):
    nc = tc.nc
    with ExitStack() as ctx:
        keep = ctx.enter_context(tc.tile_pool(name="keep", bufs=1))
        psum = ctx.enter_context(tc.psum_pool(name="psum", bufs=1))

        def sb(name, shape, dtype, tag=""):
            return keep.tile(shape, dtype, name=name, tag=tag or name, align_bytes=64)

        def bank(tag, bufs):
            return psum.tile([P, HALF], F32, name=tag, bufs=bufs)

        par_sb = keep.tile([P, S // 16], U16, name="par_sb")
        offs_sb = keep.tile([P, S // 16], U16, name="offs_sb")

        def scale_table(name, columns, engine):
            table = sb(name, [P, columns // 4], I32)
            engine.memset(table[:], 0)
            return table

        def load_scales(table, scales, first_row):
            for q in range(4):
                row = 32 * q + first_row
                nc.sync.dma_start(out=table[row : row + 4 * PASSES, :], in_=scales[:, 4 * q : 4 * q + 4, :].bitcast(I32))

        def word_table(name, words, columns, pieces, tag=""):
            table = sb(name, [P, columns], I32, tag)
            view = words.rearrange("p n t -> p (n t)").bitcast(I32)
            step = columns // pieces
            return table, [(table[:, a * step : (a + 1) * step], view[:, a * step : (a + 1) * step]) for a in range(pieces)]

        def load(pairs):
            for dst, src in pairs:
                nc.sync.dma_start(out=dst, in_=src)

        def gather_words(name, window, offsets, halves, tag=""):
            picked = sb(name, [P, halves * HALF], U32, tag)
            dealt = picked[:].rearrange("p (h s g r) -> p h g s r", h=halves, s=4, r=8)
            nc.vector.tensor_copy(out=dealt, in_=window[:].bitcast(U32).indirect(offsets))
            return picked

        def gather_scales(name, window, offsets, tag=""):
            picked = sb(name + "_listed", [P, S], U8, tag)
            nc.vector.tensor_copy(out=picked[:], in_=window[:].bitcast(U8).indirect(offsets))
            dealt = sb(name, [P, S], U8)
            nc.vector.tensor_copy(
                out=dealt[:].bitcast(I32).rearrange("p (h s g w) -> p h s g w", h=HALVES, s=4, w=2),
                in_=picked[:].bitcast(I32).rearrange("p (h g s w) -> p h s g w", h=HALVES, s=4, w=2),
            )
            return dealt

        def load_weight(name, w, g, c0, c1, pieces=1, tag=""):
            raw = sb(name, [P, PACK, c1 - c0], F32, tag)
            rows = w[g * P * PACK : (g + 1) * P * PACK, c0:c1].rearrange("(p j) n -> p j n", j=PACK)
            step = PACK // pieces
            load([(raw[:, a * step : (a + 1) * step, :], rows[:, a * step : (a + 1) * step, :]) for a in range(pieces)])
            return raw

        def quantize(name, grouped, columns, tag=""):
            codes = sb(name + "_codes", [P, columns], U32, tag)
            scales = sb(name + "_scales", [P, columns], U8)
            nc.vector.quantize_mx(out=codes[:].bitcast(FP8X4), scales=scales[:], in_=grouped)
            return codes, scales

        def round_weight(grouped, raw, c0, c1, copy):
            copy(
                out=grouped[:, c0 * PACK : c1 * PACK].rearrange("p (c i j) -> p c j i", i=4, j=PACK),
                in_=raw[:, :, c0:c1].rearrange("p j (c i) -> p c j i", i=4),
            )

        def quantize_weight(name, raw, on_vector=0, tag=""):
            grouped = sb(name + "_bf16", [P, N * PACK], BF16, tag)
            if on_vector < N:
                round_weight(grouped, raw, 0, N - on_vector, nc.scalar.copy)
            if on_vector:
                round_weight(grouped, raw, N - on_vector, N, nc.vector.tensor_copy)
            return quantize(name, grouped[:], N)

        small_rows = sb("small_rows", [P, HALVES * P], F32)
        nc.gpsimd.memset(small_rows[:], 0.0)
        e_scale_table = scale_table("e_scale_table", W, nc.gpsimd)
        x_scale_table = scale_table("x_scale_table", T, nc.vector)
        wgt_cols = sb("wgt_cols", [P, S // P], F32)
        ident = sb("ident", [P, P], F32)
        make_identity(nc, ident[:])

        e_loads = [word_table("e_table%d" % g, e_words[g], W, 4) for g in range(PASSES)]
        e_tables = [table for table, pairs in e_loads]
        nc.sync.dma_start(out=wgt_cols[:], in_=wgt.rearrange("(p c) o -> p (c o)", p=P))
        nc.sync.dma_start(out=par_sb[:], in_=par)
        load(e_loads[0][1])
        load(e_loads[1][1])
        nc.sync.dma_start(
            out=small_rows[0:4, :].rearrange("s (g r) -> s g r", r=8),
            in_=inv.rearrange("(g s r) o -> s g (r o)", s=4, r=8),
        )
        nc.sync.dma_start(out=small_rows[4 : 4 + TILES, 0:P], in_=mean[0:1, :].rearrange("o (c n) -> (o c) n", c=TILES))
        wb_raw = [load_weight("wb_raw0", wb, 0, 0, N, 2)]
        load_scales(e_scale_table, e_scales, 8)
        nc.sync.dma_start(out=offs_sb[:], in_=offs)
        wb_raw.append(load_weight("wb_raw1", wb, 1, 0, N))
        wa_raw0 = sb("wa_raw0", [P, PACK, N], F32)
        wa_rows0 = wa[0 : P * PACK, :].rearrange("(p j) n -> p j n", j=PACK)
        for g in range(PASSES):
            for q in range(4):
                row = 32 * q + 4 * g
                nc.sync.dma_start(out=x_scale_table[row : row + 4, :], in_=x_scales[g, 4 * q : 4 * q + 4, :].bitcast(I32))
            nc.sync.dma_start(out=wa_raw0[:, 2 * g : 2 * g + 2, :], in_=wa_rows0[:, 2 * g : 2 * g + 2, :])

        wgt_row = sb("wgt_row", [P, S], F32)
        wgt_view = wgt_row[:].rearrange("q (h u g b c e) -> q b u h g c e", h=HALVES, u=2, b=2, c=4, e=2)
        for b in range(2):
            spread = bank("mm", 4)
            for c in range(4):
                col = 4 * b + c
                nc.tensor.transpose(spread[:, c * P : (c + 1) * P], wgt_cols[:, col : col + 1].to_broadcast([P, P]), ident[:])
            spread_view = spread[:].rearrange("q (c h g e u) -> q u h g c e", c=4, h=HALVES, e=2, u=2)
            for u in range(2):
                nc.scalar.copy(out=wgt_view[:, b, u], in_=spread_view[:, u])

        small_turned = bank("turn", 2)
        for h in range(HALVES):
            nc.tensor.transpose(small_turned[:, h * P : (h + 1) * P], small_rows[:, h * P : (h + 1) * P], ident[:])
        small_cols = sb("small_cols", [P, HALVES, 8], F32)
        nc.scalar.copy(out=small_cols[:], in_=small_turned[:, 0 : HALVES * P].rearrange("p (h r) -> p h r", h=HALVES)[:, :, 0:8])

        def mx(acc, lhs, lhs_scale, rhs, rhs_scale, step, steps):
            nc.tensor.matmul_mx(
                out=acc,
                lhsT=lhs.bitcast(FP8X4),
                lhsT_scale=lhs_scale,
                rhs=rhs.bitcast(FP8X4),
                rhs_scale=rhs_scale,
                start=(step == 0),
                stop=(step == steps - 1),
            )

        e_picked = [gather_words("e_picked%d" % g, e_tables[g], par_sb[:], HALVES) for g in range(PASSES)]
        e_picked_scales = gather_scales("e_picked_scales", e_scale_table, par_sb[:])
        wb_q = [quantize_weight("wb0", wb_raw[0], 0, "wgt_cols"), quantize_weight("wb1", wb_raw[1], N // 2)]
        wa0_bf16 = sb("wa0_bf16", [P, N * PACK], BF16)
        round_weight(wa0_bf16, wa_raw0, 0, N, nc.scalar.copy)
        x_picked_scales = gather_scales("x_picked_scales", x_scale_table, offs_sb[:], "wb1_bf16")
        wa_q0 = quantize("wa0", wa0_bf16[:], N, "x_scale_table")
        x_loads = [word_table("x_table%d" % g, x_words[g], T, 1, "e_table%d" % g) for g in range(PASSES)]
        x_tables = [table for table, pairs in x_loads]
        load(x_loads[0][1])
        load(x_loads[1][1])
        wa_raw1 = [load_weight("wa_raw1_%d" % a, wa, 1, a * 2 * P, (a + 1) * 2 * P, 1, "wb_raw%d" % a) for a in range(2)]
        lam_pairs = [sb("lam%d" % a, [P, 2, N], F32, ("wgt_cols", "wa0_bf16")[a]) for a in range(2)]
        for a in range(2):
            nc.sync.dma_start(out=lam_pairs[a][:], in_=lam[a * 2 * P : (a + 1) * 2 * P, :].rearrange("(c p) m -> p c m", p=P))
        lam_sb = [lam_pairs[c // 2][:, c % 2, :] for c in range(TILES)]
        x_picked0 = gather_words("x_picked0", x_tables[0], offs_sb[:], HALVES, "wb1_bf16")

        vv_q = []
        for h in range(HALVES):
            planes = sb("vv_planes%d" % h, [P, PACK, N], BF16, ("wa_raw0", "vv_planes1")[h])
            for s in range(4):
                acc = bank("mm", 4)
                ts = slice(h * HALF + s * P, h * HALF + (s + 1) * P)
                for g in range(PASSES):
                    mx(acc[:], e_picked[g][:, ts], e_picked_scales[8 + 4 * g : P, ts], wb_q[g][0][:], wb_q[g][1][:], g, PASSES)
                slot = 2 * (s % 2) + s // 2
                nc.scalar.activation(out=planes[:, slot, :], in_=acc[:], func=COPY, scale=small_cols[:, h, s : s + 1])
            grouped = sb("vv_grouped%d" % h, [P, N * PACK], BF16, ("e_table0", "vv_grouped1")[h])
            round_weight(grouped, planes, 0, N, (nc.vector.tensor_copy, nc.scalar.copy)[h])
            vv_q.append(quantize("vv%d" % h, grouped[:], N))

        goal_sb = sb("goal_sb", [P, TILES, P], F32, "e_picked0")
        for c in range(TILES):
            nc.sync.dma_start(out=goal_sb[:, c, :], in_=goal[c * P : (c + 1) * P, c * P : (c + 1) * P])
        cols_per_half = HALF // 16
        x_picked1 = sb("x_picked1", [P, S], U32, "e_table0")
        for h in range(HALVES):
            dealt = x_picked1[:, h * HALF : (h + 1) * HALF].rearrange("p (s g r) -> p g s r", s=4, r=8)
            offsets = offs_sb[:, h * cols_per_half : (h + 1) * cols_per_half]
            nc.vector.tensor_copy(out=dealt, in_=x_tables[1][:].bitcast(U32).indirect(offsets))

        wa1_bf16 = sb("wa1_bf16", [P, N * PACK], BF16, "vv_planes1")

        def project(c):
            grouped = wa1_bf16[:, (c // 2) * 2 * HALF : (c // 2 + 1) * 2 * HALF]
            round_weight(grouped, wa_raw1[c // 2], (c % 2) * P, (c % 2 + 1) * P, nc.scalar.copy)
            wa_q1 = quantize("wa1_%d" % c, wa1_bf16[:, c * HALF : (c + 1) * HALF], P)
            cs = slice(c * P, (c + 1) * P)
            halves = []
            for h in range(HALVES):
                acc = bank("mm", 4)
                ts = slice(h * HALF, (h + 1) * HALF)
                mx(acc[:], wa_q0[0][:, cs], wa_q0[1][:, cs], x_picked0[:, ts], x_picked_scales[0:P, ts], 0, PASSES)
                mx(acc[:], wa_q1[0][:], wa_q1[1][:], x_picked1[:, ts], x_picked_scales[4:P, ts], 1, PASSES)
                at = sb("aT_%d_%d" % (c, h), [P, HALF], BF16)
                nc.vector.scalar_tensor_tensor(
                    out=at[:].rearrange("i (q e) -> i q e", e=2),
                    in0=acc[:].rearrange("i (e q) -> i q e", e=2),
                    scalar=small_cols[:, 0, 4 + c : 5 + c],
                    in1=wgt_row[:, ts].rearrange("i (q e) -> i q e", e=2),
                    op0=SUB,
                    op1=MULT,
                )
                halves.append(at)
            return halves

        def turn(c, halves):
            turned = bank("turn", 2)
            for h in range(HALVES):
                words = halves[h][:].bitcast(F32)
                for u in range(2):
                    slot = 2 * h + u
                    nc.tensor.transpose(turned[:, slot * P : (slot + 1) * P], words[:, u * P : (u + 1) * P], ident[:])
            a_grouped = sb("a_grouped%d" % c, [P, HALVES * P * PACK], BF16)
            nc.scalar.copy(
                out=a_grouped[:].bitcast(F32).rearrange("p (h i u) -> p h i u", h=HALVES, u=2),
                in_=turned[:].rearrange("p (h u i) -> p h i u", h=HALVES, u=2),
            )
            return a_grouped

        def correlate(c, a_grouped):
            a_codes, a_scales = quantize("a%d" % c, a_grouped[:], HALVES * P)
            z = bank("z", 2)
            for h in range(HALVES):
                hs = slice(h * P, (h + 1) * P)
                mx(z[:], a_codes[:, hs], a_scales[:, hs], vv_q[h][0][:], vv_q[h][1][:], h, HALVES)
            return z

        def finish(c, z):
            diag = slice(c * P, (c + 1) * P)
            goal_lam = sb("goal_lam%d" % c, [P, P], F32)
            nc.gpsimd.tensor_tensor(out=goal_lam[:], in0=goal_sb[:, c, :], in1=lam_sb[c][:, diag], op=MULT)
            res = sb("res%d" % c, [P, N], F32)
            nc.vector.tensor_tensor(out=res[:], in0=z[:], in1=lam_sb[c], op=MULT)
            nc.vector.tensor_tensor(out=res[:, diag], in0=res[:, diag], in1=goal_lam[:], op=SUB)
            nc.sync.dma_start(out=out[diag, :], in_=res[:])

        for c in range(TILES):
            finish(c, correlate(c, turn(c, project(c))))
